import numpy as np
import ml_dtypes


def mxq(x, axis, fmt="e4m3"):
    dtype, down = {"e4m3": (ml_dtypes.float8_e4m3fn, 7), "e5m2": (ml_dtypes.float8_e5m2, 14)}[fmt]
    v = np.moveaxis(np.asarray(x, np.float32).astype(ml_dtypes.bfloat16).astype(np.float64), axis, -1)
    blocks = v.reshape(v.shape[:-1] + (-1, 32))
    amax = np.abs(blocks).max(-1, keepdims=True)
    byte = np.maximum(np.where(amax > 0, np.frexp(amax)[1] - 1 + 127, 0) - down, 1)
    scale = np.exp2(byte - 127.0)
    codes = (blocks / scale).astype(np.float32).astype(dtype).astype(np.float64)
    return np.moveaxis((codes * scale).reshape(v.shape), -1, axis)


WIDE = False


def mx_kscale(k):
    if not WIDE:
        return np.ones(k)
    levels = np.array([10, -10, 5, -5, 0])
    if k % 512:
        return np.exp2(np.random.permutation(np.resize(levels, k // 32))).repeat(32)
    a = np.empty((k // 512, 16))
    for p in range(k // 512):
        a[p, :8] = np.random.permutation(np.resize(levels, 8))
        for g in range(8):
            far = levels[np.abs(levels - a[p, g]) >= 10]
            a[p, g + 8] = far[np.random.randint(len(far))]
    return np.exp2(a.ravel()).repeat(32)


def f64(x):
    return np.asarray(x).astype(np.float64)


def striped(idx):
    return np.tile(idx.reshape(-1, 16).T, (8, 1)).astype(np.uint16)


def unstriped(offs):
    return offs[:16].T.reshape(-1).astype(np.int64)


def silu(v):
    return v / (1.0 + np.exp(-np.maximum(v, -700.0)))


K, T, D, S, V, N = 512, 2048, 4, 2048, 512, 256


def setup_inputs():
    n = np.random.standard_normal
    s = mx_kscale(K)[:, None]
    return {
        "xT": (n((K, T)) * s).astype(np.float32),
        "w": (n((D, K, N)) / np.sqrt(D * K) / s[None]).astype(np.float32),
        "b": (0.3 * n((N, 1))).astype(np.float32),
        "gate": np.tile(np.random.uniform(0.2, 1.0, S), (N, 1)).astype(np.float32),
        "offs": striped(np.random.permutation(T)[:S]),
    }


def reference(xT, w, b, gate, offs):
    idx = unstriped(offs)
    xq = mxq(f64(xT)[:, idx], 0, "e4m3")
    wq = mxq(f64(w), 1, "e4m3")
    y = sum(wq[d].T @ xq[:, d * V:(d + 1) * V] for d in range(D))
    y = silu(y + f64(b))
    out = np.zeros((N, T))
    out[:, idx] = f64(gate) * np.tile(y, (1, D))
    return out

@@ -1,0 +1,141 @@
+from contextlib import ExitStack
+
+import concourse.mybir as mybir
+
+K, T, D, V, N = 512, 2048, 4, 512, 256
+P = 128
+J = 4
+HALVES = N // P
+STRETCH = 256
+STRETCHES = V // STRETCH
+LANES = 16
+
+FLOPS = 2 * N * V * D * K
+
+F32 = mybir.dt.float32
+BF16 = mybir.dt.bfloat16
+U32 = mybir.dt.uint32
+U16 = mybir.dt.uint16
+U8 = mybir.dt.uint8
+FP8X4 = mybir.dt.float8_e4m3fn_x4
+MULT = mybir.AluOpType.mult
+SILU = mybir.ActivationFunctionType.Silu
+
+CHUNKS = ((0, 512), (512, 512), (1024, 512), (1536, 256), (1792, 256))
+VECTOR_SHARE = {512: 352, 256: 176}
+
+
+def tile_picked_tome_lin_silu_sub_e_kernel(tc, xT, w, b, gate, offs, out):
+    nc = tc.nc
+    with ExitStack() as ctx:
+        keep = ctx.enter_context(tc.tile_pool(name="keep", bufs=1))
+        psum = ctx.enter_context(tc.psum_pool(name="psum", bufs=1))
+
+        offsets = keep.tile([P, D * V // LANES], U16, name="offsets")
+        words = keep.tile([P, T], U32, align_bytes=64, name="words")
+        scales = keep.tile([P, T], U8, align_bytes=64, name="scales")
+        bias = keep.tile([P, HALVES], F32, name="bias")
+        warm = keep.tile([P, 1], F32, name="warm")
+
+        nc.vector.memset(warm[:], 0.0)
+        nc.scalar.activation(warm[:], warm[:], SILU)
+        nc.gpsimd.memset(scales[:], 0)
+
+        x_rows = xT.rearrange("(p j) t -> p j t", j=J)
+        x_raw = []
+        for i, (t0, n) in enumerate(CHUNKS):
+            raw = keep.tile([P, J, n], F32, name=f"x_raw{i}")
+            nc.sync.dma_start(out=raw[:], in_=x_rows[:, :, t0 : t0 + n])
+            x_raw.append(raw)
+            if i == 0:
+                nc.sync.dma_start(offsets[:], offs)
+        w_raw = []
+        for d in range(D):
+            raw = keep.tile([P, J, N], F32, name=f"w_raw{d}")
+            nc.sync.dma_start(out=raw[:], in_=w[d].rearrange("(p j) m -> p j m", j=J))
+            w_raw.append(raw)
+        nc.sync.dma_start(out=bias[:], in_=b.rearrange("(h p) o -> p (h o)", p=P))
+        gates = keep.tile([P, D * V], F32, name="gates")
+        for i in range(2):
+            cols = slice(i * D * V // 2, (i + 1) * D * V // 2)
+            nc.sync.dma_start(out=gates[:, cols], in_=gate[0:P, cols])
+
+        for i, (t0, n) in enumerate(CHUNKS):
+            grouped = keep.tile([P, n, J], BF16, align_bytes=64, name=f"x_grouped{i}")
+            src = x_raw[i][:].rearrange("p j t -> p t j")
+            v = VECTOR_SHARE[n]
+            nc.scalar.copy(grouped[:, v:n, :], src[:, v:n, :])
+            nc.vector.tensor_copy(grouped[:, 0:v, :], src[:, 0:v, :])
+            nc.vector.quantize_mx(
+                out=words[:, t0 : t0 + n].bitcast(FP8X4),
+                scales=scales[:, t0 : t0 + n],
+                in_=grouped[:].rearrange("p t j -> p (t j)"),
+            )
+
+        w_codes = keep.tile([P, D, N], U32, align_bytes=64, name="w_codes")
+        w_scales = keep.tile([P, D, N], U8, align_bytes=64, name="w_scales")
+        w_grouped = []
+        for d in range(D):
+            grouped = keep.tile([P, N, J], BF16, align_bytes=64, name=f"w_grouped{d}")
+            nc.scalar.copy(grouped[:], w_raw[d][:].rearrange("p j m -> p m j"))
+            w_grouped.append(grouped)
+
+        picked = []
+        picked_scales = []
+        for s in range(STRETCHES):
+            codes_s = []
+            scales_s = []
+            for d in range(D):
+                e0 = d * V + s * STRETCH
+                entries = slice(e0 // LANES, (e0 + STRETCH) // LANES)
+                cw = keep.tile([P, STRETCH], U32, align_bytes=64, name=f"picked{s}{d}")
+                cs = keep.tile([P, STRETCH], U8, align_bytes=64, name=f"picked_scales{s}{d}")
+                nc.vector.tensor_copy(cw[:], words[:].indirect(offsets[:, entries]))
+                nc.vector.tensor_copy(cs[:], scales[:].indirect(offsets[:, entries]))
+                codes_s.append(cw)
+                scales_s.append(cs)
+                if s == 0:
+                    nc.vector.quantize_mx(
+                        out=w_codes[:, d, :].bitcast(FP8X4),
+                        scales=w_scales[:, d, :],
+                        in_=w_grouped[d][:].rearrange("p m j -> p (m j)"),
+                    )
+            picked.append(codes_s)
+            picked_scales.append(scales_s)
+
+        y = []
+        for h in range(HALVES):
+            y_h = keep.tile([P, V], F32, name=f"y{h}")
+            y.append(y_h)
+        for s in range(STRETCHES):
+            for h in range(HALVES):
+                acc = psum.tile([P, STRETCH], F32, name=f"acc{s}{h}")
+                m = slice(h * P, (h + 1) * P)
+                for d in range(D):
+                    nc.tensor.matmul_mx(
+                        out=acc[:],
+                        lhsT=w_codes[:, d, m].bitcast(FP8X4),
+                        lhsT_scale=w_scales[:, d, m],
+                        rhs=picked[s][d][:].bitcast(FP8X4),
+                        rhs_scale=picked_scales[s][d][:],
+                        start=(d == 0),
+                        stop=(d == D - 1),
+                    )
+                nc.scalar.activation(
+                    y[h][:, s * STRETCH : (s + 1) * STRETCH], acc[:], SILU, bias=bias[:, h : h + 1]
+                )
+
+        for h in range(HALVES):
+            window = keep.tile([P, T], F32, name=f"window{h}")
+            step = STRETCH if h == 0 else V
+            for v0 in range(0, V, step):
+                for d in range(D):
+                    e0 = d * V + v0
+                    entries = slice(e0 // LANES, (e0 + step) // LANES)
+                    nc.vector.tensor_tensor(
+                        window[:].indirect(offsets[:, entries]),
+                        y[h][:, v0 : v0 + step],
+                        gates[:, e0 : e0 + step],
+                        MULT,
+                    )
+            nc.sync.dma_start(out=out[h * P : (h + 1) * P, :], in_=window[:])

@@ -19,10 +19,13 @@ U16 = mybir.dt.uint16
 U8 = mybir.dt.uint8
 FP8X4 = mybir.dt.float8_e4m3fn_x4
 MULT = mybir.AluOpType.mult
+ADD = mybir.AluOpType.add
 SILU = mybir.ActivationFunctionType.Silu
+COPY = mybir.ActivationFunctionType.Copy
 
-CHUNKS = ((0, 512), (512, 512), (1024, 512), (1536, 256), (1792, 256))
-VECTOR_SHARE = {512: 352, 256: 176}
+VECTOR_GATHERS = tuple((0, d, j) for d in (0, 1) for j in range(J)) + ((1, 0, 0), (1, 0, 1))
+GPSIMD_PLANES = (0, 1)
+GPSIMD_W = (0, 1, 2)
 
 
 def tile_picked_tome_lin_silu_sub_e_kernel(tc, xT, w, b, gate, offs, out):
@@ -32,110 +35,145 @@ def tile_picked_tome_lin_silu_sub_e_kernel(tc, xT, w, b, gate, offs, out):
         psum = ctx.enter_context(tc.psum_pool(name="psum", bufs=1))
 
         offsets = keep.tile([P, D * V // LANES], U16, name="offsets")
-        words = keep.tile([P, T], U32, align_bytes=64, name="words")
-        scales = keep.tile([P, T], U8, align_bytes=64, name="scales")
         bias = keep.tile([P, HALVES], F32, name="bias")
         warm = keep.tile([P, 1], F32, name="warm")
-
         nc.vector.memset(warm[:], 0.0)
         nc.scalar.activation(warm[:], warm[:], SILU)
-        nc.gpsimd.memset(scales[:], 0)
 
         x_rows = xT.rearrange("(p j) t -> p j t", j=J)
-        x_raw = []
-        for i, (t0, n) in enumerate(CHUNKS):
-            raw = keep.tile([P, J, n], F32, name=f"x_raw{i}")
-            nc.sync.dma_start(out=raw[:], in_=x_rows[:, :, t0 : t0 + n])
-            x_raw.append(raw)
-            if i == 0:
+        x_f32 = []
+        for j in range(J):
+            plane = keep.tile([P, T], F32, name=f"x_f32_{j}")
+            nc.sync.dma_start(out=plane[:], in_=x_rows[:, j, :])
+            x_f32.append(plane)
+            if j == 0:
                 nc.sync.dma_start(offsets[:], offs)
+        nc.sync.dma_start(out=bias[:], in_=b.rearrange("(h p) o -> p (h o)", p=P))
         w_raw = []
         for d in range(D):
             raw = keep.tile([P, J, N], F32, name=f"w_raw{d}")
             nc.sync.dma_start(out=raw[:], in_=w[d].rearrange("(p j) m -> p j m", j=J))
             w_raw.append(raw)
-        nc.sync.dma_start(out=bias[:], in_=b.rearrange("(h p) o -> p (h o)", p=P))
-        gates = keep.tile([P, D * V], F32, name="gates")
-        for i in range(2):
-            cols = slice(i * D * V // 2, (i + 1) * D * V // 2)
-            nc.sync.dma_start(out=gates[:, cols], in_=gate[0:P, cols])
+        gate_view = gate[0:P, :].rearrange("p (d s v) -> p s d v", d=D, s=STRETCHES)
+        gates = []
+        for s in range(STRETCHES):
+            g = keep.tile([P, D, STRETCH], F32, name=f"gates{s}")
+            nc.sync.dma_start(out=g[:], in_=gate_view[:, s])
+            gates.append(g)
 
-        for i, (t0, n) in enumerate(CHUNKS):
-            grouped = keep.tile([P, n, J], BF16, align_bytes=64, name=f"x_grouped{i}")
-            src = x_raw[i][:].rearrange("p j t -> p t j")
-            v = VECTOR_SHARE[n]
-            nc.scalar.copy(grouped[:, v:n, :], src[:, v:n, :])
-            nc.vector.tensor_copy(grouped[:, 0:v, :], src[:, 0:v, :])
+        def entries(s, d):
+            e0 = d * V + s * STRETCH
+            return offsets[:, e0 // LANES : (e0 + STRETCH) // LANES]
+
+        grouped = {}
+        for d in range(D):
+            grouped[(0, d)] = keep.tile([P, STRETCH, J], BF16, align_bytes=64, name=f"grouped0{d}")[:]
+
+        x_b16 = []
+        for j in range(J):
+            plane = keep.tile([P, T], BF16, name=f"x_b16_{j}")
+            x_b16.append(plane)
+
+        def gather(s, d, j):
+            if (s, d, j) in VECTOR_GATHERS:
+                nc.vector.tensor_copy(grouped[(s, d)][:, :, j], x_f32[j][:].indirect(entries(s, d)))
+            else:
+                nc.scalar.activation(grouped[(s, d)][:, :, j], x_b16[j][:].indirect(entries(s, d)), COPY)
+
+        for j in range(J):
+            if j in GPSIMD_PLANES:
+                nc.gpsimd.tensor_scalar(x_b16[j][:], x_f32[j][:], 1.0, 0.0, MULT, ADD)
+            else:
+                nc.vector.tensor_copy(x_b16[j][:], x_f32[j][:])
+            for d in range(D):
+                gather(0, d, j)
+
+        codes = {}
+        scales = {}
+
+        def quantize(s, d):
+            codes[(s, d)] = keep.tile([P, STRETCH], U32, align_bytes=64, name=f"codes{s}{d}")
+            scales[(s, d)] = keep.tile([P, STRETCH], U8, align_bytes=64, name=f"scales{s}{d}")
             nc.vector.quantize_mx(
-                out=words[:, t0 : t0 + n].bitcast(FP8X4),
-                scales=scales[:, t0 : t0 + n],
-                in_=grouped[:].rearrange("p t j -> p (t j)"),
+                out=codes[(s, d)][:].bitcast(FP8X4),
+                scales=scales[(s, d)][:],
+                in_=grouped[(s, d)].rearrange("p v j -> p (v j)"),
             )
 
         w_codes = keep.tile([P, D, N], U32, align_bytes=64, name="w_codes")
         w_scales = keep.tile([P, D, N], U8, align_bytes=64, name="w_scales")
-        w_grouped = []
         for d in range(D):
-            grouped = keep.tile([P, N, J], BF16, align_bytes=64, name=f"w_grouped{d}")
-            nc.scalar.copy(grouped[:], w_raw[d][:].rearrange("p j m -> p m j"))
-            w_grouped.append(grouped)
+            w_grouped = keep.tile([P, N, J], BF16, align_bytes=64, name=f"w_grouped{d}")
+            src = w_raw[d][:].rearrange("p j m -> p m j")
+            if d in GPSIMD_W:
+                nc.gpsimd.tensor_scalar(w_grouped[:], src, 1.0, 0.0, MULT, ADD)
+            else:
+                nc.vector.tensor_copy(w_grouped[:], src)
+            nc.vector.quantize_mx(
+                out=w_codes[:, d, :].bitcast(FP8X4),
+                scales=w_scales[:, d, :],
+                in_=w_grouped[:].rearrange("p m j -> p (m j)"),
+            )
 
-        picked = []
-        picked_scales = []
-        for s in range(STRETCHES):
-            codes_s = []
-            scales_s = []
-            for d in range(D):
-                e0 = d * V + s * STRETCH
-                entries = slice(e0 // LANES, (e0 + STRETCH) // LANES)
-                cw = keep.tile([P, STRETCH], U32, align_bytes=64, name=f"picked{s}{d}")
-                cs = keep.tile([P, STRETCH], U8, align_bytes=64, name=f"picked_scales{s}{d}")
-                nc.vector.tensor_copy(cw[:], words[:].indirect(offsets[:, entries]))
-                nc.vector.tensor_copy(cs[:], scales[:].indirect(offsets[:, entries]))
-                codes_s.append(cw)
-                scales_s.append(cs)
-                if s == 0:
-                    nc.vector.quantize_mx(
-                        out=w_codes[:, d, :].bitcast(FP8X4),
-                        scales=w_scales[:, d, :],
-                        in_=w_grouped[d][:].rearrange("p m j -> p (m j)"),
-                    )
-            picked.append(codes_s)
-            picked_scales.append(scales_s)
-
-        y = []
-        for h in range(HALVES):
-            y_h = keep.tile([P, V], F32, name=f"y{h}")
-            y.append(y_h)
-        for s in range(STRETCHES):
-            for h in range(HALVES):
-                acc = psum.tile([P, STRETCH], F32, name=f"acc{s}{h}")
-                m = slice(h * P, (h + 1) * P)
-                for d in range(D):
-                    nc.tensor.matmul_mx(
-                        out=acc[:],
-                        lhsT=w_codes[:, d, m].bitcast(FP8X4),
-                        lhsT_scale=w_scales[:, d, m],
-                        rhs=picked[s][d][:].bitcast(FP8X4),
-                        rhs_scale=picked_scales[s][d][:],
-                        start=(d == 0),
-                        stop=(d == D - 1),
-                    )
-                nc.scalar.activation(
-                    y[h][:, s * STRETCH : (s + 1) * STRETCH], acc[:], SILU, bias=bias[:, h : h + 1]
-                )
-
+        windows = []
         for h in range(HALVES):
             window = keep.tile([P, T], F32, name=f"window{h}")
-            step = STRETCH if h == 0 else V
-            for v0 in range(0, V, step):
-                for d in range(D):
-                    e0 = d * V + v0
-                    entries = slice(e0 // LANES, (e0 + step) // LANES)
-                    nc.vector.tensor_tensor(
-                        window[:].indirect(offsets[:, entries]),
-                        y[h][:, v0 : v0 + step],
-                        gates[:, e0 : e0 + step],
-                        MULT,
-                    )
-            nc.sync.dma_start(out=out[h * P : (h + 1) * P, :], in_=window[:])
+            windows.append(window)
+
+        later_bias = keep.tile([P, 1], F32, align_bytes=64, name="later")
+        nc.gpsimd.tensor_copy(later_bias[:], bias[:, 0:1])
+
+        accs = {}
+
+        def multiply(h, s):
+            accs[(h, s)] = psum.tile([P, STRETCH], F32, name=f"acc{h}{s}")
+            m = slice(h * P, (h + 1) * P)
+            for d in range(D):
+                nc.tensor.matmul_mx(
+                    out=accs[(h, s)][:],
+                    lhsT=w_codes[:, d, m].bitcast(FP8X4),
+                    lhsT_scale=w_scales[:, d, m],
+                    rhs=codes[(s, d)][:].bitcast(FP8X4),
+                    rhs_scale=scales[(s, d)][:],
+                    start=(d == 0),
+                    stop=(d == D - 1),
+                )
+
+        def activate(y, h, s, bias_column):
+            nc.scalar.activation(y[:], accs[(h, s)][:], SILU, bias=bias_column)
+
+        def scatter(y, h, s, members):
+            for d in members:
+                nc.vector.tensor_tensor(windows[h][:].indirect(entries(s, d)), y[:], gates[s][:, d, :], MULT)
+
+        y = {}
+        for h in range(HALVES):
+            for s in range(STRETCHES):
+                y[(h, s)] = keep.tile([P, STRETCH], F32, name=f"y{h}{s}")
+
+        for d in range(D):
+            quantize(0, d)
+        multiply(0, 0)
+        activate(y[(0, 0)], 0, 0, later_bias[:])
+        scatter(y[(0, 0)], 0, 0, range(D))
+        multiply(1, 0)
+        activate(y[(1, 0)], 1, 0, bias[:, 1:2])
+        scatter(y[(1, 0)], 1, 0, range(2))
+
+        first = keep.tile([P, STRETCH, J], BF16, align_bytes=64, name="grouped10")
+        grouped[(1, 0)] = first[:]
+        later = keep.tile([P, D - 1, STRETCH, J], BF16, align_bytes=64, name="later")
+        for d in range(1, D):
+            grouped[(1, d)] = later[:, d - 1]
+        for d in range(D):
+            for j in range(J):
+                gather(1, d, j)
+            quantize(1, d)
+        y_late = keep.tile([P, STRETCH], F32, align_bytes=64, name="later")
+        activate(y_late, 1, 0, bias[:, 1:2])
+        scatter(y_late, 1, 0, range(2, D))
+        for h in range(HALVES):
+            multiply(h, 1)
+            activate(y[(h, 1)], h, 1, bias[:, h : h + 1])
+            scatter(y[(h, 1)], h, 1, range(D))
+            nc.sync.dma_start(out=out[h * P : (h + 1) * P, :], in_=windows[h][:])

@@ -24,8 +24,6 @@ SILU = mybir.ActivationFunctionType.Silu
 COPY = mybir.ActivationFunctionType.Copy
 
 VECTOR_GATHERS = tuple((0, d, j) for d in (0, 1) for j in range(J)) + ((1, 0, 0), (1, 0, 1))
-GPSIMD_PLANES = (0, 1)
-GPSIMD_W = (0, 1, 2)
 
 
 def tile_picked_tome_lin_silu_sub_e_kernel(tc, xT, w, b, gate, offs, out):
@@ -40,20 +38,19 @@ def tile_picked_tome_lin_silu_sub_e_kernel(tc, xT, w, b, gate, offs, out):
         nc.vector.memset(warm[:], 0.0)
         nc.scalar.activation(warm[:], warm[:], SILU)
 
+        nc.sync.dma_start(offsets[:], offs)
         x_rows = xT.rearrange("(p j) t -> p j t", j=J)
         x_f32 = []
         for j in range(J):
             plane = keep.tile([P, T], F32, name=f"x_f32_{j}")
             nc.sync.dma_start(out=plane[:], in_=x_rows[:, j, :])
             x_f32.append(plane)
-            if j == 0:
-                nc.sync.dma_start(offsets[:], offs)
-        nc.sync.dma_start(out=bias[:], in_=b.rearrange("(h p) o -> p (h o)", p=P))
         w_raw = []
         for d in range(D):
             raw = keep.tile([P, J, N], F32, name=f"w_raw{d}")
             nc.sync.dma_start(out=raw[:], in_=w[d].rearrange("(p j) m -> p j m", j=J))
             w_raw.append(raw)
+        nc.sync.dma_start(out=bias[:], in_=b.rearrange("(h p) o -> p (h o)", p=P))
         gate_view = gate[0:P, :].rearrange("p (d s v) -> p s d v", d=D, s=STRETCHES)
         gates = []
         for s in range(STRETCHES):
@@ -65,9 +62,16 @@ def tile_picked_tome_lin_silu_sub_e_kernel(tc, xT, w, b, gate, offs, out):
             e0 = d * V + s * STRETCH
             return offsets[:, e0 // LANES : (e0 + STRETCH) // LANES]
 
-        grouped = {}
-        for d in range(D):
-            grouped[(0, d)] = keep.tile([P, STRETCH, J], BF16, align_bytes=64, name=f"grouped0{d}")[:]
+        pair01 = keep.tile([P, 2, STRETCH, J], BF16, align_bytes=64, name="pair01")
+        pair23 = keep.tile([P, 2, STRETCH, J], BF16, align_bytes=64, name="pair23")
+        first = keep.tile([P, STRETCH, J], BF16, align_bytes=64, name="first")
+        grouped = {
+            (0, 0): pair01[:, 0],
+            (0, 1): pair01[:, 1],
+            (0, 2): pair23[:, 0],
+            (0, 3): pair23[:, 1],
+            (1, 0): first[:],
+        }
 
         x_b16 = []
         for j in range(J):
@@ -81,38 +85,47 @@ def tile_picked_tome_lin_silu_sub_e_kernel(tc, xT, w, b, gate, offs, out):
                 nc.scalar.activation(grouped[(s, d)][:, :, j], x_b16[j][:].indirect(entries(s, d)), COPY)
 
         for j in range(J):
-            if j in GPSIMD_PLANES:
+            if j == 0:
+                nc.scalar.copy(x_b16[j][:], x_f32[j][:])
+            elif j == 1:
                 nc.gpsimd.tensor_scalar(x_b16[j][:], x_f32[j][:], 1.0, 0.0, MULT, ADD)
             else:
                 nc.vector.tensor_copy(x_b16[j][:], x_f32[j][:])
             for d in range(D):
                 gather(0, d, j)
+            gather(1, 0, j)
 
         codes = {}
         scales = {}
 
-        def quantize(s, d):
-            codes[(s, d)] = keep.tile([P, STRETCH], U32, align_bytes=64, name=f"codes{s}{d}")
-            scales[(s, d)] = keep.tile([P, STRETCH], U8, align_bytes=64, name=f"scales{s}{d}")
-            nc.vector.quantize_mx(
-                out=codes[(s, d)][:].bitcast(FP8X4),
-                scales=scales[(s, d)][:],
-                in_=grouped[(s, d)].rearrange("p v j -> p (v j)"),
-            )
+        def quantize(s, members, values):
+            n = len(members) * STRETCH
+            c = keep.tile([P, n], U32, align_bytes=64, name=f"codes{s}{members[0]}")
+            sc = keep.tile([P, n], U8, align_bytes=64, name=f"scales{s}{members[0]}")
+            nc.vector.quantize_mx(out=c[:].bitcast(FP8X4), scales=sc[:], in_=values)
+            for i, d in enumerate(members):
+                codes[(s, d)] = c[:, i * STRETCH : (i + 1) * STRETCH]
+                scales[(s, d)] = sc[:, i * STRETCH : (i + 1) * STRETCH]
 
-        w_codes = keep.tile([P, D, N], U32, align_bytes=64, name="w_codes")
-        w_scales = keep.tile([P, D, N], U8, align_bytes=64, name="w_scales")
+        quantize(0, (0, 1), pair01[:].rearrange("p d v j -> p (d v j)"))
+
+        w_codes = keep.tile([P, HALVES, D, P], U32, align_bytes=64, name="w_codes")
+        w_scales = keep.tile([P, HALVES, D, P], U8, align_bytes=64, name="w_scales")
+        w_grouped = keep.tile([P, HALVES, D, P, J], BF16, align_bytes=64, name="w_grouped")
         for d in range(D):
-            w_grouped = keep.tile([P, N, J], BF16, align_bytes=64, name=f"w_grouped{d}")
-            src = w_raw[d][:].rearrange("p j m -> p m j")
-            if d in GPSIMD_W:
-                nc.gpsimd.tensor_scalar(w_grouped[:], src, 1.0, 0.0, MULT, ADD)
+            src = w_raw[d][:].rearrange("p j (h m) -> p h m j", h=HALVES)
+            if d == 0:
+                nc.gpsimd.tensor_scalar(w_grouped[:, :, d], src, 1.0, 0.0, MULT, ADD)
+            elif d == 2:
+                nc.scalar.copy(w_grouped[:, :, d], src)
             else:
-                nc.vector.tensor_copy(w_grouped[:], src)
+                nc.vector.tensor_copy(w_grouped[:, :, d], src)
+        quantize(0, (2, 3), pair23[:].rearrange("p d v j -> p (d v j)"))
+        for h in range(HALVES):
             nc.vector.quantize_mx(
-                out=w_codes[:, d, :].bitcast(FP8X4),
-                scales=w_scales[:, d, :],
-                in_=w_grouped[:].rearrange("p m j -> p (m j)"),
+                out=w_codes[:, h].rearrange("p d m -> p (d m)").bitcast(FP8X4),
+                scales=w_scales[:, h].rearrange("p d m -> p (d m)"),
+                in_=w_grouped[:, h].rearrange("p d m j -> p (d m j)"),
             )
 
         windows = []
@@ -127,14 +140,13 @@ def tile_picked_tome_lin_silu_sub_e_kernel(tc, xT, w, b, gate, offs, out):
 
         def multiply(h, s):
             accs[(h, s)] = psum.tile([P, STRETCH], F32, name=f"acc{h}{s}")
-            m = slice(h * P, (h + 1) * P)
             for d in range(D):
                 nc.tensor.matmul_mx(
                     out=accs[(h, s)][:],
-                    lhsT=w_codes[:, d, m].bitcast(FP8X4),
-                    lhsT_scale=w_scales[:, d, m],
-                    rhs=codes[(s, d)][:].bitcast(FP8X4),
-                    rhs_scale=scales[(s, d)][:],
+                    lhsT=w_codes[:, h, d, :].bitcast(FP8X4),
+                    lhsT_scale=w_scales[:, h, d, :],
+                    rhs=codes[(s, d)].bitcast(FP8X4),
+                    rhs_scale=scales[(s, d)],
                     start=(d == 0),
                     stop=(d == D - 1),
                 )
@@ -151,8 +163,6 @@ def tile_picked_tome_lin_silu_sub_e_kernel(tc, xT, w, b, gate, offs, out):
             for s in range(STRETCHES):
                 y[(h, s)] = keep.tile([P, STRETCH], F32, name=f"y{h}{s}")
 
-        for d in range(D):
-            quantize(0, d)
         multiply(0, 0)
         activate(y[(0, 0)], 0, 0, later_bias[:])
         scatter(y[(0, 0)], 0, 0, range(D))
@@ -160,15 +170,15 @@ def tile_picked_tome_lin_silu_sub_e_kernel(tc, xT, w, b, gate, offs, out):
         activate(y[(1, 0)], 1, 0, bias[:, 1:2])
         scatter(y[(1, 0)], 1, 0, range(2))
 
-        first = keep.tile([P, STRETCH, J], BF16, align_bytes=64, name="grouped10")
-        grouped[(1, 0)] = first[:]
         later = keep.tile([P, D - 1, STRETCH, J], BF16, align_bytes=64, name="later")
         for d in range(1, D):
             grouped[(1, d)] = later[:, d - 1]
-        for d in range(D):
+        quantize(1, (0,), first[:].rearrange("p v j -> p (v j)"))
+        for d in range(1, D):
             for j in range(J):
                 gather(1, d, j)
-            quantize(1, d)
+            if d != 2:
+                quantize(1, (d,) if d == 1 else (2, 3), later[:, d - 1 if d == 1 else 1 : d].rearrange("p d v j -> p (d v j)"))
         y_late = keep.tile([P, STRETCH], F32, align_bytes=64, name="later")
         activate(y_late, 1, 0, bias[:, 1:2])
         scatter(y_late, 1, 0, range(2, D))

@@ -87,7 +87,7 @@ def tile_picked_tome_lin_silu_sub_e_kernel(tc, xT, w, b, gate, offs, out):
         for j in range(J):
             if j == 0:
                 nc.scalar.copy(x_b16[j][:], x_f32[j][:])
-            elif j == 1:
+            elif j % 2 == 1:
                 nc.gpsimd.tensor_scalar(x_b16[j][:], x_f32[j][:], 1.0, 0.0, MULT, ADD)
             else:
                 nc.vector.tensor_copy(x_b16[j][:], x_f32[j][:])
@@ -111,22 +111,21 @@ def tile_picked_tome_lin_silu_sub_e_kernel(tc, xT, w, b, gate, offs, out):
 
         w_codes = keep.tile([P, HALVES, D, P], U32, align_bytes=64, name="w_codes")
         w_scales = keep.tile([P, HALVES, D, P], U8, align_bytes=64, name="w_scales")
-        w_grouped = keep.tile([P, HALVES, D, P, J], BF16, align_bytes=64, name="w_grouped")
-        for d in range(D):
-            src = w_raw[d][:].rearrange("p j (h m) -> p h m j", h=HALVES)
-            if d == 0:
-                nc.gpsimd.tensor_scalar(w_grouped[:, :, d], src, 1.0, 0.0, MULT, ADD)
-            elif d == 2:
-                nc.scalar.copy(w_grouped[:, :, d], src)
-            else:
-                nc.vector.tensor_copy(w_grouped[:, :, d], src)
-        quantize(0, (2, 3), pair23[:].rearrange("p d v j -> p (d v j)"))
-        for h in range(HALVES):
+        def quantize_w(h, movers):
+            w_grouped = keep.tile([P, D, P, J], BF16, align_bytes=64, name="w_grouped")
+            for d in range(D):
+                movers[d](w_grouped[:, d], w_raw[d][:, :, h * P : (h + 1) * P].rearrange("p j m -> p m j"))
             nc.vector.quantize_mx(
                 out=w_codes[:, h].rearrange("p d m -> p (d m)").bitcast(FP8X4),
                 scales=w_scales[:, h].rearrange("p d m -> p (d m)"),
-                in_=w_grouped[:, h].rearrange("p d m j -> p (d m j)"),
+                in_=w_grouped[:].rearrange("p d m j -> p (d m j)"),
             )
+
+        def on_gpsimd(o, i):
+            nc.gpsimd.tensor_scalar(o, i, 1.0, 0.0, MULT, ADD)
+
+        quantize(0, (2, 3), pair23[:].rearrange("p d v j -> p (d v j)"))
+        quantize_w(0, (on_gpsimd, nc.vector.tensor_copy, nc.scalar.copy, nc.vector.tensor_copy))
 
         windows = []
         for h in range(HALVES):
@@ -165,6 +164,7 @@ def tile_picked_tome_lin_silu_sub_e_kernel(tc, xT, w, b, gate, offs, out):
 
         multiply(0, 0)
         activate(y[(0, 0)], 0, 0, later_bias[:])
+        quantize_w(1, (nc.vector.tensor_copy, nc.vector.tensor_copy, nc.scalar.copy, nc.vector.tensor_copy))
         scatter(y[(0, 0)], 0, 0, range(D))
         multiply(1, 0)
         activate(y[(1, 0)], 1, 0, bias[:, 1:2])

from contextlib import ExitStack

import concourse.mybir as mybir

K, T, D, V, N = 512, 2048, 4, 512, 256
P = 128
J = 4
HALVES = N // P
STRETCH = 256
STRETCHES = V // STRETCH
LANES = 16

FLOPS = 2 * N * V * D * K

F32 = mybir.dt.float32
BF16 = mybir.dt.bfloat16
U32 = mybir.dt.uint32
U16 = mybir.dt.uint16
U8 = mybir.dt.uint8
FP8X4 = mybir.dt.float8_e4m3fn_x4
MULT = mybir.AluOpType.mult
ADD = mybir.AluOpType.add
SILU = mybir.ActivationFunctionType.Silu
COPY = mybir.ActivationFunctionType.Copy

VECTOR_GATHERS = tuple((0, d, j) for d in (0, 1) for j in range(J)) + ((1, 0, 0), (1, 0, 1))


def tile_picked_tome_lin_silu_sub_e_kernel(tc, xT, w, b, gate, offs, out):
    nc = tc.nc
    with ExitStack() as ctx:
        keep = ctx.enter_context(tc.tile_pool(name="keep", bufs=1))
        psum = ctx.enter_context(tc.psum_pool(name="psum", bufs=1))

        offsets = keep.tile([P, D * V // LANES], U16, name="offsets")
        bias = keep.tile([P, HALVES], F32, name="bias")
        warm = keep.tile([P, 1], F32, name="warm")
        nc.vector.memset(warm[:], 0.0)
        nc.scalar.activation(warm[:], warm[:], SILU)

        nc.sync.dma_start(offsets[:], offs)
        x_rows = xT.rearrange("(p j) t -> p j t", j=J)
        x_f32 = []
        for j in range(J):
            plane = keep.tile([P, T], F32, name=f"x_f32_{j}")
            nc.sync.dma_start(out=plane[:], in_=x_rows[:, j, :])
            x_f32.append(plane)
        w_raw = []
        for d in range(D):
            raw = keep.tile([P, J, N], F32, name=f"w_raw{d}")
            nc.sync.dma_start(out=raw[:], in_=w[d].rearrange("(p j) m -> p j m", j=J))
            w_raw.append(raw)
        nc.sync.dma_start(out=bias[:], in_=b.rearrange("(h p) o -> p (h o)", p=P))
        gate_view = gate[0:P, :].rearrange("p (d s v) -> p s d v", d=D, s=STRETCHES)
        gates = []
        for s in range(STRETCHES):
            g = keep.tile([P, D, STRETCH], F32, name=f"gates{s}")
            nc.sync.dma_start(out=g[:], in_=gate_view[:, s])
            gates.append(g)

        def entries(s, d):
            e0 = d * V + s * STRETCH
            return offsets[:, e0 // LANES : (e0 + STRETCH) // LANES]

        pair01 = keep.tile([P, 2, STRETCH, J], BF16, align_bytes=64, name="pair01")
        pair23 = keep.tile([P, 2, STRETCH, J], BF16, align_bytes=64, name="pair23")
        first = keep.tile([P, STRETCH, J], BF16, align_bytes=64, name="first")
        grouped = {
            (0, 0): pair01[:, 0],
            (0, 1): pair01[:, 1],
            (0, 2): pair23[:, 0],
            (0, 3): pair23[:, 1],
            (1, 0): first[:],
        }

        x_b16 = []
        for j in range(J):
            plane = keep.tile([P, T], BF16, name=f"x_b16_{j}")
            x_b16.append(plane)

        def gather(s, d, j):
            if (s, d, j) in VECTOR_GATHERS:
                nc.vector.tensor_copy(grouped[(s, d)][:, :, j], x_f32[j][:].indirect(entries(s, d)))
            else:
                nc.scalar.activation(grouped[(s, d)][:, :, j], x_b16[j][:].indirect(entries(s, d)), COPY)

        for j in range(J):
            if j == 0:
                nc.scalar.copy(x_b16[j][:], x_f32[j][:])
            elif j % 2 == 1:
                nc.gpsimd.tensor_scalar(x_b16[j][:], x_f32[j][:], 1.0, 0.0, MULT, ADD)
            else:
                nc.vector.tensor_copy(x_b16[j][:], x_f32[j][:])
            for d in range(D):
                gather(0, d, j)
            gather(1, 0, j)

        codes = {}
        scales = {}

        def quantize(s, members, values):
            n = len(members) * STRETCH
            c = keep.tile([P, n], U32, align_bytes=64, name=f"codes{s}{members[0]}")
            sc = keep.tile([P, n], U8, align_bytes=64, name=f"scales{s}{members[0]}")
            nc.vector.quantize_mx(out=c[:].bitcast(FP8X4), scales=sc[:], in_=values)
            for i, d in enumerate(members):
                codes[(s, d)] = c[:, i * STRETCH : (i + 1) * STRETCH]
                scales[(s, d)] = sc[:, i * STRETCH : (i + 1) * STRETCH]

        quantize(0, (0, 1), pair01[:].rearrange("p d v j -> p (d v j)"))

        w_codes = keep.tile([P, HALVES, D, P], U32, align_bytes=64, name="w_codes")
        w_scales = keep.tile([P, HALVES, D, P], U8, align_bytes=64, name="w_scales")
        def quantize_w(h, movers):
            w_grouped = keep.tile([P, D, P, J], BF16, align_bytes=64, name="w_grouped")
            for d in range(D):
                movers[d](w_grouped[:, d], w_raw[d][:, :, h * P : (h + 1) * P].rearrange("p j m -> p m j"))
            nc.vector.quantize_mx(
                out=w_codes[:, h].rearrange("p d m -> p (d m)").bitcast(FP8X4),
                scales=w_scales[:, h].rearrange("p d m -> p (d m)"),
                in_=w_grouped[:].rearrange("p d m j -> p (d m j)"),
            )

        def on_gpsimd(o, i):
            nc.gpsimd.tensor_scalar(o, i, 1.0, 0.0, MULT, ADD)

        quantize(0, (2, 3), pair23[:].rearrange("p d v j -> p (d v j)"))
        quantize_w(0, (on_gpsimd, nc.vector.tensor_copy, nc.scalar.copy, nc.vector.tensor_copy))

        windows = []
        for h in range(HALVES):
            window = keep.tile([P, T], F32, name=f"window{h}")
            windows.append(window)

        later_bias = keep.tile([P, 1], F32, align_bytes=64, name="later")
        nc.gpsimd.tensor_copy(later_bias[:], bias[:, 0:1])

        accs = {}

        def multiply(h, s):
            accs[(h, s)] = psum.tile([P, STRETCH], F32, name=f"acc{h}{s}")
            for d in range(D):
                nc.tensor.matmul_mx(
                    out=accs[(h, s)][:],
                    lhsT=w_codes[:, h, d, :].bitcast(FP8X4),
                    lhsT_scale=w_scales[:, h, d, :],
                    rhs=codes[(s, d)].bitcast(FP8X4),
                    rhs_scale=scales[(s, d)],
                    start=(d == 0),
                    stop=(d == D - 1),
                )

        def activate(y, h, s, bias_column):
            nc.scalar.activation(y[:], accs[(h, s)][:], SILU, bias=bias_column)

        def scatter(y, h, s, members):
            for d in members:
                nc.vector.tensor_tensor(windows[h][:].indirect(entries(s, d)), y[:], gates[s][:, d, :], MULT)

        y = {}
        for h in range(HALVES):
            for s in range(STRETCHES):
                y[(h, s)] = keep.tile([P, STRETCH], F32, name=f"y{h}{s}")

        multiply(0, 0)
        activate(y[(0, 0)], 0, 0, later_bias[:])
        quantize_w(1, (nc.vector.tensor_copy, nc.vector.tensor_copy, nc.scalar.copy, nc.vector.tensor_copy))
        scatter(y[(0, 0)], 0, 0, range(D))
        multiply(1, 0)
        activate(y[(1, 0)], 1, 0, bias[:, 1:2])
        scatter(y[(1, 0)], 1, 0, range(2))

        later = keep.tile([P, D - 1, STRETCH, J], BF16, align_bytes=64, name="later")
        for d in range(1, D):
            grouped[(1, d)] = later[:, d - 1]
        quantize(1, (0,), first[:].rearrange("p v j -> p (v j)"))
        for d in range(1, D):
            for j in range(J):
                gather(1, d, j)
            if d != 2:
                quantize(1, (d,) if d == 1 else (2, 3), later[:, d - 1 if d == 1 else 1 : d].rearrange("p d v j -> p (d v j)"))
        y_late = keep.tile([P, STRETCH], F32, align_bytes=64, name="later")
        activate(y_late, 1, 0, bias[:, 1:2])
        scatter(y_late, 1, 0, range(2, D))
        for h in range(HALVES):
            multiply(h, 1)
            activate(y[(h, 1)], h, 1, bias[:, h : h + 1])
            scatter(y[(h, 1)], h, 1, range(D))
            nc.sync.dma_start(out=out[h * P : (h + 1) * P, :], in_=windows[h][:])
